import numpy as np, ml_dtypes
CORES = [5,29,101,125,133,157,229,253]
N = 8
import mx_ref
BF = ml_dtypes.bfloat16
def entries(a):
    return np.ascontiguousarray(a.T).reshape(-1)
def table(e):
    return np.ascontiguousarray(np.reshape(e, (-1, 16)).T).astype(np.int32)
def f(rng, *shape):
    return mx_ref.flush((rng.standard_normal(shape, dtype=np.float32) * np.exp2(rng.integers(-2, 3, shape[:-1] + (1,)))).astype(BF))
def wide(rng, *shape, cols=0):
    v = rng.standard_normal(shape, dtype=np.float32) * np.exp2(rng.integers(-12, 13, shape)).astype(np.float32)
    if cols: v *= np.repeat(np.exp2(rng.integers(-cols, cols + 1, shape[:-2] + (1, shape[-1] // 4))) * (rng.random(shape[:-2] + (1, shape[-1] // 4)) > 0.0625), 4, axis=-1).astype(np.float32)
    return mx_ref.flush(v.astype(BF))
NL, LO, O = 1024, 128, 2
HOST = np.array([0 if k < 128 else 1 for k in CORES])
def tables_of(s):
    return np.stack([table(e) for e in s])
def won(rng, win):
    v = rng.integers(1, 2 ** rng.integers(0, 21, NL) + 1)
    s = rng.integers(0, v, (N, NL)); s[win, np.arange(NL)] = v
    return tables_of(s)
def setup_inputs(rng):
    s = rng.integers(0, 2 ** rng.integers(0, 21, NL) + 1, (N, NL))
    return {"x": f(rng, N, 128, 4 * NL), "w": f(rng, N, 128, 512 * O), "sc": tables_of(s)}
def setup_inputs_ties(rng):
    s = np.zeros((N, NL), int)
    for q in range(N):
        for i, j in enumerate(rng.permutation(LO) + q * LO):
            a, b = [rng.permutation(np.flatnonzero(HOST == h)) for h in rng.permutation(2)]
            if i % 3 == 0: e = np.arange(N)
            elif i % 3 == 1: e = a[:rng.integers(2, len(a) + 1)]
            else: e = np.concatenate([a[:rng.integers(1, len(a) + 1)], b[:rng.integers(1, len(b) + 1)]])
            v = 0 if i == 0 else 2 ** 20 if i < 4 else int(rng.integers(1, 2 ** 20 + 1))
            s[:, j] = rng.integers(0, max(v, 1), N); s[e, j] = v
    return {**setup_inputs(rng), "sc": tables_of(s)}
def setup_inputs_close(rng):
    v = rng.integers(1, 2 ** rng.integers(0, 21, NL) + 1)
    v.reshape(N, LO)[:, rng.permutation(LO)[:2]] = [1, 2 ** 20]
    win = rng.integers(0, N, NL); second = (win + rng.integers(1, N, NL)) % N
    s = np.where(rng.random((N, NL)) < 0.5, v - 1, rng.integers(0, v, (N, NL)))
    s[second, np.arange(NL)] = v - 1; s[win, np.arange(NL)] = v
    return {**setup_inputs(rng), "sc": tables_of(s)}
def setup_inputs_most(rng):
    p = int(rng.integers(0, N))
    win = (p + rng.integers(1, N, (N, LO))) % N
    for i, q in enumerate(rng.permutation(N)):
        if i == 0: win[q] = p
        elif i > 1: win[q, rng.permutation(LO)[:-(-9 * LO // 10)]] = p
    return {**setup_inputs(rng), "sc": won(rng, win.reshape(-1))}
def setup_inputs_sides(rng):
    win = np.zeros((N, LO), int)
    for h in range(2):
        own = rng.permutation(np.flatnonzero(HOST == h))
        for i, q in enumerate(own):
            win[q] = rng.choice(np.flatnonzero(HOST == (1 - h if i < len(own) // 2 else h)), LO)
    return {**setup_inputs(rng), "sc": won(rng, win.reshape(-1))}
def setup_inputs_spread(rng):
    d = setup_inputs(rng); d["x"] = wide(rng, N, 128, 4 * NL, cols=6); return d
def check_inputs(d):
    b = []
    for r in range(N):
        s = entries(d["sc"][r])
        if s.min() < 0 or s.max() > 2 ** 20: b.append("sc")
    return b
def reference(x, w, sc):
    best = np.stack([entries(e) for e in sc]).argmax(axis=0)
    y = np.zeros((N, 128, O * LO), np.float32)
    for q in range(N):
        M = np.concatenate([x[best[l]][:, 4 * l:4 * l + 4] for l in range(q * LO, q * LO + LO)], axis=1)
        M = mx_ref.quantize(M)
        for o in range(O): y[q][:, LO * o:LO * o + LO] = mx_ref.matmul(mx_ref.quantize(w[q][:, 512 * o:512 * o + 512]), M)
    return {"y": y}

@@ -1,0 +1,244 @@
+from concourse.bass import DstId, RemoteDMATransfer
+from concourse.mybir import dt, AluOpType, ActivationFunctionType
+
+N, NL, LO, O = 8, 1024, 128, 2
+KC = LO // 16
+
+SCRATCH = {
+    "xb": ("sbuf", [128, 4 * NL], "bfloat16"),
+    "wb": ("sbuf", [128, 512 * O], "bfloat16"),
+    "sck": ("sbuf", [128, NL // 16], "int32"),
+    "key": ("sbuf", [128, NL // 16], "int32"),
+    "kin": ("sbuf", [128, KC * N], "int32"),
+    "m1": ("sbuf", [128, KC * 4], "int32"),
+    "m2": ("sbuf", [128, KC * 2], "int32"),
+    "m3": ("sbuf", [128, KC], "int32"),
+    "m4": ("sbuf", [128, KC], "int32"),
+    "m5": ("sbuf", [128, KC], "int32"),
+    "m6": ("sbuf", [128, KC], "int32"),
+    "ip": ("sbuf", [128, KC], "int32"),
+    "ic": ("sbuf", [128, KC], "int32"),
+    "jp": ("sbuf", [128, KC], "int32"),
+    "jt": ("sbuf", [128, KC], "int32"),
+    "off": ("sbuf", [128, KC], "uint16"),
+    "sq": ("sbuf", [128, NL], "float8_e4m3fn_x4"),
+    "ss": ("sbuf", [128, NL], "uint8"),
+    "rk": ("sbuf", [128, KC], "int32"),
+    "rq": ("sbuf", [128, LO], "float8_e4m3fn_x4"),
+    "rs": ("sbuf", [128, LO], "uint8"),
+    "winq": ("sbuf", [128, NL], "float8_e4m3fn_x4"),
+    "wins": ("sbuf", [128, NL], "uint8"),
+    "mq": ("sbuf", [128, LO], "float8_e4m3fn_x4"),
+    "ms": ("sbuf", [128, LO], "uint8"),
+    "wq": ("sbuf", [128, LO * O], "float8_e4m3fn_x4"),
+    "ws": ("sbuf", [128, LO * O], "uint8"),
+    "ps0": ("psum", [128, 512], "float32"),
+    "ps1": ("psum", [128, 512], "float32"),
+    "ysb": ("sbuf", [128, LO * O], "float32"),
+}
+SEMAPHORES = (["lsc", "lw", "kq", "kown", "iot", "jv", "qc", "qd", "qo", "qw", "am", "offs", "pc", "pscale",
+               "mm0", "mm1", "cp0", "cp1", "st0", "st1", "arrk", "arrq", "arrs", "rak", "raq", "ras", "left"]
+              + ["lx%d" % i for i in range(N)])
+
+
+def mask_of(engines):
+    return sum(1 << e for e in engines)
+
+
+def plan(r, cores, topo):
+    me = cores[r]
+    plane = [q for q in range(N) if q == r or topo.same_plane(me, cores[q])]
+    cross = [q for q in range(N) if q not in plane]
+    i = plane.index(r)
+    ports = [c for c in topo.cores_of(me) if c != me and all(topo.may_write(c, cores[q]) for q in cross)]
+    ports.sort(key=lambda c: (topo.die(c) != topo.die(me), c))
+    far = [c for c in topo.cores_of(me) if c != me and c not in ports and topo.die(c) != topo.die(me)]
+    relays = {q: ports[(i + k) % len(ports)] for k, q in enumerate(cross)}
+    n = len(plane)
+    via = plane[(i + 1) % n]
+    relays[via] = far[0]
+    direct = [plane[(i + 2) % n], plane[(i + 3) % n]]
+    return {"cross": cross, "via": via, "direct": direct, "relays": relays, "order": cross + [via] + direct + [r]}
+
+
+def send(dst, src, topo, engines, rsem, out, in_):
+    rid, pid = topo.addr(dst, src)
+    return RemoteDMATransfer(dst_ids=[DstId(rid=rid, pnc=pid)], dma_engine_mask=mask_of(engines), remote_sem=rsem,
+                             src=in_, dst=out)
+
+
+def relay_program(g, core, T, topo, r, q):
+    S = T.sem
+    dst = T.cores[q]
+    rid, pid = topo.addr(dst, core)
+    mask = topo.mask(core, dst)
+    eng = len(topo.engines(core, dst))
+    p = plan(r, T.cores, topo)
+    k, c = relay_engines(r, q, p, T.cores, topo)
+    slot = LO * (N - 1 - r)
+    g.wait_ge(S.rak, len(k))
+    g.remote_dma(T.kin[:, KC * r:KC * r + KC], T.rk[:, :], S.arrk, S.left, pid, rid, mask)
+    g.wait_ge(S.raq, len(c))
+    g.remote_dma(T.winq[:, slot:slot + LO].bitcast(dt.uint8), T.rq[:, 0:LO].bitcast(dt.uint8), S.arrq, S.left,
+                 pid, rid, mask)
+    g.wait_ge(S.ras, len(c))
+    g.remote_dma(T.wins[:, slot:slot + LO], T.rs[:, 0:LO], S.arrs, S.left, pid, rid, mask)
+    g.wait_ge(S.left, 3 * eng)
+
+
+def relay_engines(r, q, p, cores, topo):
+    me = cores[r]
+    order = p["order"]
+    off_chip = topo.engines(me, cores[p["direct"][0]])
+    on_chip = topo.engines(me, p["relays"][p["via"]])
+    if q in p["direct"]:
+        d = p["direct"].index(q)
+        h = len(off_chip) // 2
+        return off_chip[2 * d:2 * d + 2], off_chip[h * d:h * d + h]
+    taken = off_chip[0:2 * len(p["direct"])]
+    rest = [e for e in on_chip if e not in taken]
+    n = order.index(q)
+    keys = rest[2 * n:2 * n + 2]
+    if q == p["via"]:
+        return keys, [e for e in on_chip if e not in off_chip]
+    w = len(on_chip) // len(p["cross"])
+    return keys, on_chip[w * n:w * n + w]
+
+
+def rank_program(g, core, T, topo):
+    S = T.sem
+    rank = T.rank_of(core)
+    if rank is None:
+        for r in range(N):
+            for q, c in plan(r, T.cores, topo)["relays"].items():
+                if c == core:
+                    relay_program(g, core, T, topo, r, q)
+        return
+
+    p = plan(rank, T.cores, topo)
+    order = p["order"]
+    sy, sc, v, te = g.sync, g.scalar, g.vector, g.tensor
+
+    for i, q in enumerate(order):
+        sy.dma_start(T.xb[:, 512 * i:512 * i + 512], T.x[:, 512 * q:512 * q + 512]).then_inc(S["lx%d" % i], 16)
+    sy.dma_start(T.wb[:, :], T.w[:, :]).then_inc(S.lw, 16)
+    for h in range(8):
+        sc.dma_start(T.sck[16 * h:16 * h + 16, :], T.sc[:, :]).then_inc(S.lsc, 16)
+
+    g.iota(T.ip[:, :], [[0, KC]], 0, 1).then_inc(S.iot, 1)
+    g.iota(T.ic[:, :], [[16, KC]], 0, 0).then_inc(S.iot, 1)
+    v.wait_ge(S.iot, 2)
+    v.tensor_scalar(T.jp[:, :], T.ip[:, :], 15, None, AluOpType.bitwise_and).then_inc(S.jv, 1)
+    v.wait_ge(S.jv, 1)
+    v.tensor_tensor(T.jt[:, :], T.jp[:, :], T.ic[:, :], AluOpType.add).then_inc(S.jv, 1)
+
+    v.wait_ge(S.lsc, 16 * 8)
+    v.tensor_scalar(T.key[:, :], T.sck[:, :], N, N - 1 - rank, AluOpType.mult, AluOpType.add).then_inc(S.kq, 1)
+
+    def quant(i, oq, os, sem):
+        v.wait_ge(S["lx%d" % i], 16)
+        v.quantize_mx(oq, os, T.xb[:, 512 * i:512 * i + 512]).then_inc(sem, 1)
+
+    ncross = len(p["cross"])
+    for i in range(N - 1):
+        quant(i, T.sq[:, LO * i:LO * i + LO], T.ss[:, LO * i:LO * i + LO], S.qc if i < ncross else S.qd)
+    v.tensor_scalar(T.kin[:, KC * rank:KC * rank + KC], T.sck[:, KC * rank:KC * rank + KC], N, N - 1 - rank,
+                    AluOpType.mult, AluOpType.add).then_inc(S.kown, 1)
+    mine = LO * (N - 1 - rank)
+    quant(N - 1, T.winq[:, mine:mine + LO], T.wins[:, mine:mine + LO], S.qo)
+    v.wait_ge(S.lw, 16)
+    v.quantize_mx(T.wq[:, :], T.ws[:, :], T.wb[:, :]).then_inc(S.qw, 1)
+
+    left = [0]
+
+    def transfers(kind, qs):
+        out = []
+        for q in qs:
+            i = order.index(q)
+            ke, ce = relay_engines(rank, q, p, T.cores, topo)
+            e = ke if kind == "k" else ce
+            far = q in p["relays"]
+            dst = p["relays"][q] if far else T.cores[q]
+            if kind == "k":
+                src = T.key[:, KC * q:KC * q + KC]
+                to = T.rk[:, :] if far else T.kin[:, KC * rank:KC * rank + KC]
+                rsem = S.rak if far else S.arrk
+            elif kind == "q":
+                src = T.sq[:, LO * i:LO * i + LO].bitcast(dt.uint8)
+                to = (T.rq[:, 0:LO] if far else T.winq[:, mine:mine + LO]).bitcast(dt.uint8)
+                rsem = S.raq if far else S.arrq
+            else:
+                src = T.ss[:, LO * i:LO * i + LO]
+                to = T.rs[:, 0:LO] if far else T.wins[:, mine:mine + LO]
+                rsem = S.ras if far else S.arrs
+            out.append(send(dst, core, topo, e, rsem, to, src))
+            left[0] += len(e)
+        return out
+
+    rest = [p["via"]] + p["direct"]
+    g.wait_ge(S.kq, 1)
+    g.remote_dma_fused(transfers("k", order[:N - 1]), local_sem=S.left)
+    g.wait_ge(S.qc, ncross)
+    g.remote_dma_fused(transfers("q", p["cross"]), local_sem=S.left)
+    g.remote_dma_fused(transfers("s", p["cross"]), local_sem=S.left)
+    g.wait_ge(S.qd, len(rest))
+    g.remote_dma_fused(transfers("q", rest), local_sem=S.left)
+    g.remote_dma_fused(transfers("s", rest), local_sem=S.left)
+
+    nk = nc = 0
+    for r in range(N):
+        if r == rank:
+            continue
+        pr = plan(r, T.cores, topo)
+        if rank in pr["relays"]:
+            e = len(topo.engines(pr["relays"][rank], core))
+            nk, nc = nk + e, nc + e
+        else:
+            ke, ce = relay_engines(r, rank, pr, T.cores, topo)
+            nk, nc = nk + len(ke), nc + len(ce)
+
+    v.wait_ge(S.arrk, nk)
+    v.wait_ge(S.kown, 1)
+    v.tensor_tensor(T.m1[:, :], T.kin[:, 0:4 * KC], T.kin[:, 4 * KC:8 * KC], AluOpType.max).then_inc(S.am, 1)
+    v.wait_ge(S.am, 1)
+    v.tensor_tensor(T.m2[:, :], T.m1[:, 0:2 * KC], T.m1[:, 2 * KC:4 * KC], AluOpType.max).then_inc(S.am, 1)
+    v.wait_ge(S.am, 2)
+    v.tensor_tensor(T.m3[:, :], T.m2[:, 0:KC], T.m2[:, KC:2 * KC], AluOpType.max).then_inc(S.am, 1)
+    v.wait_ge(S.am, 3)
+    v.tensor_scalar(T.m4[:, :], T.m3[:, :], N - 1, None, AluOpType.bitwise_and).then_inc(S.am, 1)
+    v.wait_ge(S.am, 4)
+    v.tensor_scalar(T.m5[:, :], T.m4[:, :], LO, None, AluOpType.mult).then_inc(S.am, 1)
+    v.wait_ge(S.am, 5)
+    v.wait_ge(S.jv, 2)
+    v.tensor_tensor(T.m6[:, :], T.m5[:, :], T.jt[:, :], AluOpType.add).then_inc(S.am, 1)
+    v.wait_ge(S.am, 6)
+    v.tensor_copy(T.off[:, :], T.m6[:, :]).then_inc(S.offs, 1)
+
+    v.wait_ge(S.offs, 1)
+    v.wait_ge(S.qo, 1)
+    v.wait_ge(S.arrq, nc)
+    v.tensor_copy(T.mq[:, 0:LO].bitcast(dt.uint32),
+                  T.winq[:, 0:NL].bitcast(dt.uint32).indirect(T.off[:, 0:KC])).then_inc(S.pc, 1)
+    sc.wait_ge(S.offs, 1)
+    sc.wait_ge(S.qo, 1)
+    sc.wait_ge(S.arrs, nc)
+    sc.activation(T.ms[:, 0:LO], T.wins[:, 0:NL].indirect(T.off[:, 0:KC]),
+                  ActivationFunctionType.Copy).then_inc(S.pscale, 1)
+
+    te.wait_ge(S.qw, 1)
+    te.wait_ge(S.pc, 1)
+    te.wait_ge(S.pscale, 1)
+    for o, (ps, mm) in enumerate(((T.ps0, S.mm0), (T.ps1, S.mm1))):
+        te.matmul_mx(ps[:, 0:LO], T.wq[:, LO * o:LO * o + LO], T.ws[:, LO * o:LO * o + LO], T.mq[:, 0:LO],
+                     T.ms[:, 0:LO], True, True).then_inc(mm, 1)
+    v.wait_ge(S.mm0, 1)
+    v.tensor_copy(T.ysb[:, 0:LO], T.ps0[:, 0:LO]).then_inc(S.cp0, 1)
+    sc.wait_ge(S.mm1, 1)
+    sc.activation(T.ysb[:, LO:2 * LO], T.ps1[:, 0:LO], ActivationFunctionType.Copy).then_inc(S.cp1, 1)
+    sy.wait_ge(S.cp0, 1)
+    sy.dma_start(T.y[:, 0:LO], T.ysb[:, 0:LO]).then_inc(S.st0, 16)
+    sc.wait_ge(S.cp1, 1)
+    sc.dma_start(T.y[:, LO:2 * LO], T.ysb[:, LO:2 * LO]).then_inc(S.st1, 16)
+    sy.wait_ge(S.st0, 16)
+    sc.wait_ge(S.st1, 16)
+    g.wait_ge(S.left, left[0])

@@ -8,8 +8,10 @@ SCRATCH = {
     "xb": ("sbuf", [128, 4 * NL], "bfloat16"),
     "wb": ("sbuf", [128, 512 * O], "bfloat16"),
     "sck": ("sbuf", [128, NL // 16], "int32"),
-    "key": ("sbuf", [128, NL // 16], "int32"),
     "kin": ("sbuf", [128, KC * N], "int32"),
+    "kin8": ("sbuf", [128, KC * N], "int32"),
+    "slot": ("sbuf", [128, KC * N], "int32"),
+    "m0": ("sbuf", [128, KC * N], "int32"),
     "m1": ("sbuf", [128, KC * 4], "int32"),
     "m2": ("sbuf", [128, KC * 2], "int32"),
     "m3": ("sbuf", [128, KC], "int32"),
@@ -36,7 +38,7 @@ SCRATCH = {
     "ps1": ("psum", [128, 512], "float32"),
     "ysb": ("sbuf", [128, LO * O], "float32"),
 }
-SEMAPHORES = (["lsc", "lw", "kq", "kown", "iot", "jv", "qc", "qd", "qo", "qw", "am", "offs", "pc", "pscale",
+SEMAPHORES = (["lsc", "lw", "kown", "iot", "jv", "qg0", "qg1", "qo", "qw", "am", "offs", "pc", "pscale",
                "mm0", "mm1", "cp0", "cp1", "st0", "st1", "arrk", "arrq", "arrs", "rak", "raq", "ras", "left"]
               + ["lx%d" % i for i in range(N)])
 
@@ -49,22 +51,25 @@ def plan(r, cores, topo):
     me = cores[r]
     plane = [q for q in range(N) if q == r or topo.same_plane(me, cores[q])]
     cross = [q for q in range(N) if q not in plane]
-    i = plane.index(r)
+    i, n = plane.index(r), len(plane)
     ports = [c for c in topo.cores_of(me) if c != me and all(topo.may_write(c, cores[q]) for q in cross)]
     ports.sort(key=lambda c: (topo.die(c) != topo.die(me), c))
     far = [c for c in topo.cores_of(me) if c != me and c not in ports and topo.die(c) != topo.die(me)]
     relays = {q: ports[(i + k) % len(ports)] for k, q in enumerate(cross)}
-    n = len(plane)
     via = plane[(i + 1) % n]
     relays[via] = far[0]
     direct = [plane[(i + 2) % n], plane[(i + 3) % n]]
-    return {"cross": cross, "via": via, "direct": direct, "relays": relays, "order": cross + [via] + direct + [r]}
-
-
-def send(dst, src, topo, engines, rsem, out, in_):
-    rid, pid = topo.addr(dst, src)
-    return RemoteDMATransfer(dst_ids=[DstId(rid=rid, pnc=pid)], dma_engine_mask=mask_of(engines), remote_sem=rsem,
-                             src=in_, dst=out)
+    groups = [cross, [via] + direct]
+    out = topo.engines(me, cores[direct[0]])
+    on = topo.engines(me, far[0])
+    f, h = len(on) // 4, len(out) // 2
+    cols = {q: on[f * k:f * k + f] for k, q in enumerate(cross)}
+    cols.update({via: [e for e in on if e not in out], direct[0]: out[:h], direct[1]: out[h:]})
+    keys = {direct[0]: out[0:2], direct[1]: out[2:4]}
+    rest = [e for e in on if e not in out[0:4]]
+    for k, q in enumerate(cross + [via]):
+        keys[q] = rest[2 * k:2 * k + 2]
+    return {"groups": groups, "order": groups[0] + groups[1] + [r], "relays": relays, "keys": keys, "cols": cols}
 
 
 def relay_program(g, core, T, topo, r, q):
@@ -72,37 +77,16 @@ def relay_program(g, core, T, topo, r, q):
     dst = T.cores[q]
     rid, pid = topo.addr(dst, core)
     mask = topo.mask(core, dst)
-    eng = len(topo.engines(core, dst))
     p = plan(r, T.cores, topo)
-    k, c = relay_engines(r, q, p, T.cores, topo)
     slot = LO * (N - 1 - r)
-    g.wait_ge(S.rak, len(k))
+    g.wait_ge(S.rak, len(p["keys"][q]))
     g.remote_dma(T.kin[:, KC * r:KC * r + KC], T.rk[:, :], S.arrk, S.left, pid, rid, mask)
-    g.wait_ge(S.raq, len(c))
+    g.wait_ge(S.raq, len(p["cols"][q]))
     g.remote_dma(T.winq[:, slot:slot + LO].bitcast(dt.uint8), T.rq[:, 0:LO].bitcast(dt.uint8), S.arrq, S.left,
                  pid, rid, mask)
-    g.wait_ge(S.ras, len(c))
+    g.wait_ge(S.ras, len(p["cols"][q]))
     g.remote_dma(T.wins[:, slot:slot + LO], T.rs[:, 0:LO], S.arrs, S.left, pid, rid, mask)
-    g.wait_ge(S.left, 3 * eng)
-
-
-def relay_engines(r, q, p, cores, topo):
-    me = cores[r]
-    order = p["order"]
-    off_chip = topo.engines(me, cores[p["direct"][0]])
-    on_chip = topo.engines(me, p["relays"][p["via"]])
-    if q in p["direct"]:
-        d = p["direct"].index(q)
-        h = len(off_chip) // 2
-        return off_chip[2 * d:2 * d + 2], off_chip[h * d:h * d + h]
-    taken = off_chip[0:2 * len(p["direct"])]
-    rest = [e for e in on_chip if e not in taken]
-    n = order.index(q)
-    keys = rest[2 * n:2 * n + 2]
-    if q == p["via"]:
-        return keys, [e for e in on_chip if e not in off_chip]
-    w = len(on_chip) // len(p["cross"])
-    return keys, on_chip[w * n:w * n + w]
+    g.wait_ge(S.left, 3 * len(topo.engines(core, dst)))
 
 
 def rank_program(g, core, T, topo):
@@ -119,31 +103,32 @@ def rank_program(g, core, T, topo):
     order = p["order"]
     sy, sc, v, te = g.sync, g.scalar, g.vector, g.tensor
 
-    for i, q in enumerate(order):
-        sy.dma_start(T.xb[:, 512 * i:512 * i + 512], T.x[:, 512 * q:512 * q + 512]).then_inc(S["lx%d" % i], 16)
-    sy.dma_start(T.wb[:, :], T.w[:, :]).then_inc(S.lw, 16)
+    two = (sy, sc)
     for h in range(8):
-        sc.dma_start(T.sck[16 * h:16 * h + 16, :], T.sc[:, :]).then_inc(S.lsc, 16)
+        two[h % 2].dma_start(T.sck[16 * h:16 * h + 16, :], T.sc[:, :]).then_inc(S.lsc, 16)
+    for i, q in enumerate(order):
+        two[i % 2].dma_start(T.xb[:, 512 * i:512 * i + 512], T.x[:, 512 * q:512 * q + 512]).then_inc(S["lx%d" % i], 16)
+    sy.dma_start(T.wb[:, :], T.w[:, :]).then_inc(S.lw, 16)
 
     g.iota(T.ip[:, :], [[0, KC]], 0, 1).then_inc(S.iot, 1)
     g.iota(T.ic[:, :], [[16, KC]], 0, 0).then_inc(S.iot, 1)
-    v.wait_ge(S.iot, 2)
+    g.iota(T.slot[:, :], [[-1, N], [0, KC]], N - 1, 0).then_inc(S.iot, 1)
+    v.wait_ge(S.iot, 3)
     v.tensor_scalar(T.jp[:, :], T.ip[:, :], 15, None, AluOpType.bitwise_and).then_inc(S.jv, 1)
     v.wait_ge(S.jv, 1)
     v.tensor_tensor(T.jt[:, :], T.jp[:, :], T.ic[:, :], AluOpType.add).then_inc(S.jv, 1)
-
-    v.wait_ge(S.lsc, 16 * 8)
-    v.tensor_scalar(T.key[:, :], T.sck[:, :], N, N - 1 - rank, AluOpType.mult, AluOpType.add).then_inc(S.kq, 1)
 
     def quant(i, oq, os, sem):
         v.wait_ge(S["lx%d" % i], 16)
         v.quantize_mx(oq, os, T.xb[:, 512 * i:512 * i + 512]).then_inc(sem, 1)
 
-    ncross = len(p["cross"])
-    for i in range(N - 1):
-        quant(i, T.sq[:, LO * i:LO * i + LO], T.ss[:, LO * i:LO * i + LO], S.qc if i < ncross else S.qd)
-    v.tensor_scalar(T.kin[:, KC * rank:KC * rank + KC], T.sck[:, KC * rank:KC * rank + KC], N, N - 1 - rank,
-                    AluOpType.mult, AluOpType.add).then_inc(S.kown, 1)
+    i = 0
+    for n, group in enumerate(p["groups"]):
+        for q in group:
+            quant(i, T.sq[:, LO * i:LO * i + LO], T.ss[:, LO * i:LO * i + LO], S["qg%d" % n])
+            i += 1
+    v.wait_ge(S.lsc, 16 * 8)
+    v.tensor_copy(T.kin[:, KC * rank:KC * rank + KC], T.sck[:, KC * rank:KC * rank + KC]).then_inc(S.kown, 1)
     mine = LO * (N - 1 - rank)
     quant(N - 1, T.winq[:, mine:mine + LO], T.wins[:, mine:mine + LO], S.qo)
     v.wait_ge(S.lw, 16)
@@ -151,16 +136,14 @@ def rank_program(g, core, T, topo):
 
     left = [0]
 
-    def transfers(kind, qs):
+    def send(kind, qs):
         out = []
         for q in qs:
             i = order.index(q)
-            ke, ce = relay_engines(rank, q, p, T.cores, topo)
-            e = ke if kind == "k" else ce
             far = q in p["relays"]
             dst = p["relays"][q] if far else T.cores[q]
             if kind == "k":
-                src = T.key[:, KC * q:KC * q + KC]
+                src = T.sck[:, KC * q:KC * q + KC]
                 to = T.rk[:, :] if far else T.kin[:, KC * rank:KC * rank + KC]
                 rsem = S.rak if far else S.arrk
             elif kind == "q":
@@ -171,19 +154,19 @@ def rank_program(g, core, T, topo):
                 src = T.ss[:, LO * i:LO * i + LO]
                 to = T.rs[:, 0:LO] if far else T.wins[:, mine:mine + LO]
                 rsem = S.ras if far else S.arrs
-            out.append(send(dst, core, topo, e, rsem, to, src))
+            e = p["keys" if kind == "k" else "cols"][q]
+            rid, pid = topo.addr(dst, core)
+            out.append(RemoteDMATransfer(dst_ids=[DstId(rid=rid, pnc=pid)], dma_engine_mask=mask_of(e),
+                                         remote_sem=rsem, src=src, dst=to))
             left[0] += len(e)
-        return out
+        g.remote_dma_fused(out, local_sem=S.left)
 
-    rest = [p["via"]] + p["direct"]
-    g.wait_ge(S.kq, 1)
-    g.remote_dma_fused(transfers("k", order[:N - 1]), local_sem=S.left)
-    g.wait_ge(S.qc, ncross)
-    g.remote_dma_fused(transfers("q", p["cross"]), local_sem=S.left)
-    g.remote_dma_fused(transfers("s", p["cross"]), local_sem=S.left)
-    g.wait_ge(S.qd, len(rest))
-    g.remote_dma_fused(transfers("q", rest), local_sem=S.left)
-    g.remote_dma_fused(transfers("s", rest), local_sem=S.left)
+    g.wait_ge(S.lsc, 16 * 8)
+    send("k", order[:N - 1])
+    for n, group in enumerate(p["groups"]):
+        g.wait_ge(S["qg%d" % n], len(group))
+        send("q", group)
+        send("s", group)
 
     nk = nc = 0
     for r in range(N):
@@ -194,24 +177,27 @@ def rank_program(g, core, T, topo):
             e = len(topo.engines(pr["relays"][rank], core))
             nk, nc = nk + e, nc + e
         else:
-            ke, ce = relay_engines(r, rank, pr, T.cores, topo)
-            nk, nc = nk + len(ke), nc + len(ce)
+            nk, nc = nk + len(pr["keys"][rank]), nc + len(pr["cols"][rank])
 
     v.wait_ge(S.arrk, nk)
     v.wait_ge(S.kown, 1)
-    v.tensor_tensor(T.m1[:, :], T.kin[:, 0:4 * KC], T.kin[:, 4 * KC:8 * KC], AluOpType.max).then_inc(S.am, 1)
+    v.tensor_scalar(T.kin8[:, :], T.kin[:, :], N, None, AluOpType.mult).then_inc(S.am, 1)
     v.wait_ge(S.am, 1)
-    v.tensor_tensor(T.m2[:, :], T.m1[:, 0:2 * KC], T.m1[:, 2 * KC:4 * KC], AluOpType.max).then_inc(S.am, 1)
+    v.tensor_tensor(T.m0[:, :], T.kin8[:, :], T.slot[:, :], AluOpType.add).then_inc(S.am, 1)
     v.wait_ge(S.am, 2)
-    v.tensor_tensor(T.m3[:, :], T.m2[:, 0:KC], T.m2[:, KC:2 * KC], AluOpType.max).then_inc(S.am, 1)
+    v.tensor_tensor(T.m1[:, :], T.m0[:, 0:4 * KC], T.m0[:, 4 * KC:8 * KC], AluOpType.max).then_inc(S.am, 1)
     v.wait_ge(S.am, 3)
-    v.tensor_scalar(T.m4[:, :], T.m3[:, :], N - 1, None, AluOpType.bitwise_and).then_inc(S.am, 1)
+    v.tensor_tensor(T.m2[:, :], T.m1[:, 0:2 * KC], T.m1[:, 2 * KC:4 * KC], AluOpType.max).then_inc(S.am, 1)
     v.wait_ge(S.am, 4)
-    v.tensor_scalar(T.m5[:, :], T.m4[:, :], LO, None, AluOpType.mult).then_inc(S.am, 1)
+    v.tensor_tensor(T.m3[:, :], T.m2[:, 0:KC], T.m2[:, KC:2 * KC], AluOpType.max).then_inc(S.am, 1)
     v.wait_ge(S.am, 5)
+    v.tensor_scalar(T.m4[:, :], T.m3[:, :], N - 1, None, AluOpType.bitwise_and).then_inc(S.am, 1)
+    v.wait_ge(S.am, 6)
+    v.tensor_scalar(T.m5[:, :], T.m4[:, :], LO, None, AluOpType.mult).then_inc(S.am, 1)
+    v.wait_ge(S.am, 7)
     v.wait_ge(S.jv, 2)
     v.tensor_tensor(T.m6[:, :], T.m5[:, :], T.jt[:, :], AluOpType.add).then_inc(S.am, 1)
-    v.wait_ge(S.am, 6)
+    v.wait_ge(S.am, 8)
     v.tensor_copy(T.off[:, :], T.m6[:, :]).then_inc(S.offs, 1)
 
     v.wait_ge(S.offs, 1)

@@ -16,12 +16,12 @@ SCRATCH = {
     "m2": ("sbuf", [128, KC * 2], "int32"),
     "m3": ("sbuf", [128, KC], "int32"),
     "m4": ("sbuf", [128, KC], "int32"),
-    "m5": ("sbuf", [128, KC], "int32"),
-    "m6": ("sbuf", [128, KC], "int32"),
+    "m5": ("sbuf", [128, KC], "float32"),
     "ip": ("sbuf", [128, KC], "int32"),
     "ic": ("sbuf", [128, KC], "int32"),
     "jp": ("sbuf", [128, KC], "int32"),
     "jt": ("sbuf", [128, KC], "int32"),
+    "jf": ("sbuf", [128, KC], "float32"),
     "off": ("sbuf", [128, KC], "uint16"),
     "sq": ("sbuf", [128, NL], "float8_e4m3fn_x4"),
     "ss": ("sbuf", [128, NL], "uint8"),
@@ -108,6 +108,7 @@ def rank_program(g, core, T, topo):
         two[h % 2].dma_start(T.sck[16 * h:16 * h + 16, :], T.sc[:, :]).then_inc(S.lsc, 16)
     for i, q in enumerate(order):
         two[i % 2].dma_start(T.xb[:, 512 * i:512 * i + 512], T.x[:, 512 * q:512 * q + 512]).then_inc(S["lx%d" % i], 16)
+    sy.wait_ge(S["lx%d" % (N - 2)], 16)
     sy.dma_start(T.wb[:, :], T.w[:, :]).then_inc(S.lw, 16)
 
     g.iota(T.ip[:, :], [[0, KC]], 0, 1).then_inc(S.iot, 1)
@@ -117,6 +118,8 @@ def rank_program(g, core, T, topo):
     v.tensor_scalar(T.jp[:, :], T.ip[:, :], 15, None, AluOpType.bitwise_and).then_inc(S.jv, 1)
     v.wait_ge(S.jv, 1)
     v.tensor_tensor(T.jt[:, :], T.jp[:, :], T.ic[:, :], AluOpType.add).then_inc(S.jv, 1)
+    v.wait_ge(S.jv, 2)
+    v.tensor_scalar(T.jf[:, :], T.jt[:, :], 1.0 / LO, None, AluOpType.mult).then_inc(S.jv, 1)
 
     def quant(i, oq, os, sem):
         v.wait_ge(S["lx%d" % i], 16)
@@ -131,8 +134,6 @@ def rank_program(g, core, T, topo):
     v.tensor_copy(T.kin[:, KC * rank:KC * rank + KC], T.sck[:, KC * rank:KC * rank + KC]).then_inc(S.kown, 1)
     mine = LO * (N - 1 - rank)
     quant(N - 1, T.winq[:, mine:mine + LO], T.wins[:, mine:mine + LO], S.qo)
-    v.wait_ge(S.lw, 16)
-    v.quantize_mx(T.wq[:, :], T.ws[:, :], T.wb[:, :]).then_inc(S.qw, 1)
 
     left = [0]
 
@@ -193,12 +194,13 @@ def rank_program(g, core, T, topo):
     v.wait_ge(S.am, 5)
     v.tensor_scalar(T.m4[:, :], T.m3[:, :], N - 1, None, AluOpType.bitwise_and).then_inc(S.am, 1)
     v.wait_ge(S.am, 6)
-    v.tensor_scalar(T.m5[:, :], T.m4[:, :], LO, None, AluOpType.mult).then_inc(S.am, 1)
+    v.wait_ge(S.jv, 3)
+    v.tensor_tensor(T.m5[:, :], T.m4[:, :], T.jf[:, :], AluOpType.add).then_inc(S.am, 1)
     v.wait_ge(S.am, 7)
-    v.wait_ge(S.jv, 2)
-    v.tensor_tensor(T.m6[:, :], T.m5[:, :], T.jt[:, :], AluOpType.add).then_inc(S.am, 1)
-    v.wait_ge(S.am, 8)
-    v.tensor_copy(T.off[:, :], T.m6[:, :]).then_inc(S.offs, 1)
+    v.tensor_scalar(T.off[:, :], T.m5[:, :], float(LO), None, AluOpType.mult).then_inc(S.offs, 1)
+
+    v.wait_ge(S.lw, 16)
+    v.quantize_mx(T.wq[:, :], T.ws[:, :], T.wb[:, :]).then_inc(S.qw, 1)
 
     v.wait_ge(S.offs, 1)
     v.wait_ge(S.qo, 1)

from concourse.bass import DstId, RemoteDMATransfer
from concourse.mybir import dt, AluOpType, ActivationFunctionType

N, NL, LO, O = 8, 1024, 128, 2
KC = LO // 16

SCRATCH = {
    "xb": ("sbuf", [128, 4 * NL], "bfloat16"),
    "wb": ("sbuf", [128, 512 * O], "bfloat16"),
    "sck": ("sbuf", [128, NL // 16], "int32"),
    "kin": ("sbuf", [128, KC * N], "int32"),
    "kin8": ("sbuf", [128, KC * N], "int32"),
    "slot": ("sbuf", [128, KC * N], "int32"),
    "m0": ("sbuf", [128, KC * N], "int32"),
    "m1": ("sbuf", [128, KC * 4], "int32"),
    "m2": ("sbuf", [128, KC * 2], "int32"),
    "m3": ("sbuf", [128, KC], "int32"),
    "m4": ("sbuf", [128, KC], "int32"),
    "m5": ("sbuf", [128, KC], "float32"),
    "ip": ("sbuf", [128, KC], "int32"),
    "ic": ("sbuf", [128, KC], "int32"),
    "jp": ("sbuf", [128, KC], "int32"),
    "jt": ("sbuf", [128, KC], "int32"),
    "jf": ("sbuf", [128, KC], "float32"),
    "off": ("sbuf", [128, KC], "uint16"),
    "sq": ("sbuf", [128, NL], "float8_e4m3fn_x4"),
    "ss": ("sbuf", [128, NL], "uint8"),
    "rk": ("sbuf", [128, KC], "int32"),
    "rq": ("sbuf", [128, LO], "float8_e4m3fn_x4"),
    "rs": ("sbuf", [128, LO], "uint8"),
    "winq": ("sbuf", [128, NL], "float8_e4m3fn_x4"),
    "wins": ("sbuf", [128, NL], "uint8"),
    "mq": ("sbuf", [128, LO], "float8_e4m3fn_x4"),
    "ms": ("sbuf", [128, LO], "uint8"),
    "wq": ("sbuf", [128, LO * O], "float8_e4m3fn_x4"),
    "ws": ("sbuf", [128, LO * O], "uint8"),
    "ps0": ("psum", [128, 512], "float32"),
    "ps1": ("psum", [128, 512], "float32"),
    "ysb": ("sbuf", [128, LO * O], "float32"),
}
SEMAPHORES = (["lsc", "lw", "kown", "iot", "jv", "qg0", "qg1", "qo", "qw", "am", "offs", "pc", "pscale",
               "mm0", "mm1", "cp0", "cp1", "st0", "st1", "arrk", "arrq", "arrs", "rak", "raq", "ras", "left"]
              + ["lx%d" % i for i in range(N)])


def mask_of(engines):
    return sum(1 << e for e in engines)


def plan(r, cores, topo):
    me = cores[r]
    plane = [q for q in range(N) if q == r or topo.same_plane(me, cores[q])]
    cross = [q for q in range(N) if q not in plane]
    i, n = plane.index(r), len(plane)
    ports = [c for c in topo.cores_of(me) if c != me and all(topo.may_write(c, cores[q]) for q in cross)]
    ports.sort(key=lambda c: (topo.die(c) != topo.die(me), c))
    far = [c for c in topo.cores_of(me) if c != me and c not in ports and topo.die(c) != topo.die(me)]
    relays = {q: ports[(i + k) % len(ports)] for k, q in enumerate(cross)}
    via = plane[(i + 1) % n]
    relays[via] = far[0]
    direct = [plane[(i + 2) % n], plane[(i + 3) % n]]
    groups = [cross, [via] + direct]
    out = topo.engines(me, cores[direct[0]])
    on = topo.engines(me, far[0])
    f, h = len(on) // 4, len(out) // 2
    cols = {q: on[f * k:f * k + f] for k, q in enumerate(cross)}
    cols.update({via: [e for e in on if e not in out], direct[0]: out[:h], direct[1]: out[h:]})
    keys = {direct[0]: out[0:2], direct[1]: out[2:4]}
    rest = [e for e in on if e not in out[0:4]]
    for k, q in enumerate(cross + [via]):
        keys[q] = rest[2 * k:2 * k + 2]
    return {"groups": groups, "order": groups[0] + groups[1] + [r], "relays": relays, "keys": keys, "cols": cols}


def relay_program(g, core, T, topo, r, q):
    S = T.sem
    dst = T.cores[q]
    rid, pid = topo.addr(dst, core)
    mask = topo.mask(core, dst)
    p = plan(r, T.cores, topo)
    slot = LO * (N - 1 - r)
    g.wait_ge(S.rak, len(p["keys"][q]))
    g.remote_dma(T.kin[:, KC * r:KC * r + KC], T.rk[:, :], S.arrk, S.left, pid, rid, mask)
    g.wait_ge(S.raq, len(p["cols"][q]))
    g.remote_dma(T.winq[:, slot:slot + LO].bitcast(dt.uint8), T.rq[:, 0:LO].bitcast(dt.uint8), S.arrq, S.left,
                 pid, rid, mask)
    g.wait_ge(S.ras, len(p["cols"][q]))
    g.remote_dma(T.wins[:, slot:slot + LO], T.rs[:, 0:LO], S.arrs, S.left, pid, rid, mask)
    g.wait_ge(S.left, 3 * len(topo.engines(core, dst)))


def rank_program(g, core, T, topo):
    S = T.sem
    rank = T.rank_of(core)
    if rank is None:
        for r in range(N):
            for q, c in plan(r, T.cores, topo)["relays"].items():
                if c == core:
                    relay_program(g, core, T, topo, r, q)
        return

    p = plan(rank, T.cores, topo)
    order = p["order"]
    sy, sc, v, te = g.sync, g.scalar, g.vector, g.tensor

    two = (sy, sc)
    for h in range(8):
        two[h % 2].dma_start(T.sck[16 * h:16 * h + 16, :], T.sc[:, :]).then_inc(S.lsc, 16)
    for i, q in enumerate(order):
        two[i % 2].dma_start(T.xb[:, 512 * i:512 * i + 512], T.x[:, 512 * q:512 * q + 512]).then_inc(S["lx%d" % i], 16)
    sy.wait_ge(S["lx%d" % (N - 2)], 16)
    sy.dma_start(T.wb[:, :], T.w[:, :]).then_inc(S.lw, 16)

    g.iota(T.ip[:, :], [[0, KC]], 0, 1).then_inc(S.iot, 1)
    g.iota(T.ic[:, :], [[16, KC]], 0, 0).then_inc(S.iot, 1)
    g.iota(T.slot[:, :], [[-1, N], [0, KC]], N - 1, 0).then_inc(S.iot, 1)
    v.wait_ge(S.iot, 3)
    v.tensor_scalar(T.jp[:, :], T.ip[:, :], 15, None, AluOpType.bitwise_and).then_inc(S.jv, 1)
    v.wait_ge(S.jv, 1)
    v.tensor_tensor(T.jt[:, :], T.jp[:, :], T.ic[:, :], AluOpType.add).then_inc(S.jv, 1)
    v.wait_ge(S.jv, 2)
    v.tensor_scalar(T.jf[:, :], T.jt[:, :], 1.0 / LO, None, AluOpType.mult).then_inc(S.jv, 1)

    def quant(i, oq, os, sem):
        v.wait_ge(S["lx%d" % i], 16)
        v.quantize_mx(oq, os, T.xb[:, 512 * i:512 * i + 512]).then_inc(sem, 1)

    i = 0
    for n, group in enumerate(p["groups"]):
        for q in group:
            quant(i, T.sq[:, LO * i:LO * i + LO], T.ss[:, LO * i:LO * i + LO], S["qg%d" % n])
            i += 1
    v.wait_ge(S.lsc, 16 * 8)
    v.tensor_copy(T.kin[:, KC * rank:KC * rank + KC], T.sck[:, KC * rank:KC * rank + KC]).then_inc(S.kown, 1)
    mine = LO * (N - 1 - rank)
    quant(N - 1, T.winq[:, mine:mine + LO], T.wins[:, mine:mine + LO], S.qo)

    left = [0]

    def send(kind, qs):
        out = []
        for q in qs:
            i = order.index(q)
            far = q in p["relays"]
            dst = p["relays"][q] if far else T.cores[q]
            if kind == "k":
                src = T.sck[:, KC * q:KC * q + KC]
                to = T.rk[:, :] if far else T.kin[:, KC * rank:KC * rank + KC]
                rsem = S.rak if far else S.arrk
            elif kind == "q":
                src = T.sq[:, LO * i:LO * i + LO].bitcast(dt.uint8)
                to = (T.rq[:, 0:LO] if far else T.winq[:, mine:mine + LO]).bitcast(dt.uint8)
                rsem = S.raq if far else S.arrq
            else:
                src = T.ss[:, LO * i:LO * i + LO]
                to = T.rs[:, 0:LO] if far else T.wins[:, mine:mine + LO]
                rsem = S.ras if far else S.arrs
            e = p["keys" if kind == "k" else "cols"][q]
            rid, pid = topo.addr(dst, core)
            out.append(RemoteDMATransfer(dst_ids=[DstId(rid=rid, pnc=pid)], dma_engine_mask=mask_of(e),
                                         remote_sem=rsem, src=src, dst=to))
            left[0] += len(e)
        g.remote_dma_fused(out, local_sem=S.left)

    g.wait_ge(S.lsc, 16 * 8)
    send("k", order[:N - 1])
    for n, group in enumerate(p["groups"]):
        g.wait_ge(S["qg%d" % n], len(group))
        send("q", group)
        send("s", group)

    nk = nc = 0
    for r in range(N):
        if r == rank:
            continue
        pr = plan(r, T.cores, topo)
        if rank in pr["relays"]:
            e = len(topo.engines(pr["relays"][rank], core))
            nk, nc = nk + e, nc + e
        else:
            nk, nc = nk + len(pr["keys"][rank]), nc + len(pr["cols"][rank])

    v.wait_ge(S.arrk, nk)
    v.wait_ge(S.kown, 1)
    v.tensor_scalar(T.kin8[:, :], T.kin[:, :], N, None, AluOpType.mult).then_inc(S.am, 1)
    v.wait_ge(S.am, 1)
    v.tensor_tensor(T.m0[:, :], T.kin8[:, :], T.slot[:, :], AluOpType.add).then_inc(S.am, 1)
    v.wait_ge(S.am, 2)
    v.tensor_tensor(T.m1[:, :], T.m0[:, 0:4 * KC], T.m0[:, 4 * KC:8 * KC], AluOpType.max).then_inc(S.am, 1)
    v.wait_ge(S.am, 3)
    v.tensor_tensor(T.m2[:, :], T.m1[:, 0:2 * KC], T.m1[:, 2 * KC:4 * KC], AluOpType.max).then_inc(S.am, 1)
    v.wait_ge(S.am, 4)
    v.tensor_tensor(T.m3[:, :], T.m2[:, 0:KC], T.m2[:, KC:2 * KC], AluOpType.max).then_inc(S.am, 1)
    v.wait_ge(S.am, 5)
    v.tensor_scalar(T.m4[:, :], T.m3[:, :], N - 1, None, AluOpType.bitwise_and).then_inc(S.am, 1)
    v.wait_ge(S.am, 6)
    v.wait_ge(S.jv, 3)
    v.tensor_tensor(T.m5[:, :], T.m4[:, :], T.jf[:, :], AluOpType.add).then_inc(S.am, 1)
    v.wait_ge(S.am, 7)
    v.tensor_scalar(T.off[:, :], T.m5[:, :], float(LO), None, AluOpType.mult).then_inc(S.offs, 1)

    v.wait_ge(S.lw, 16)
    v.quantize_mx(T.wq[:, :], T.ws[:, :], T.wb[:, :]).then_inc(S.qw, 1)

    v.wait_ge(S.offs, 1)
    v.wait_ge(S.qo, 1)
    v.wait_ge(S.arrq, nc)
    v.tensor_copy(T.mq[:, 0:LO].bitcast(dt.uint32),
                  T.winq[:, 0:NL].bitcast(dt.uint32).indirect(T.off[:, 0:KC])).then_inc(S.pc, 1)
    sc.wait_ge(S.offs, 1)
    sc.wait_ge(S.qo, 1)
    sc.wait_ge(S.arrs, nc)
    sc.activation(T.ms[:, 0:LO], T.wins[:, 0:NL].indirect(T.off[:, 0:KC]),
                  ActivationFunctionType.Copy).then_inc(S.pscale, 1)

    te.wait_ge(S.qw, 1)
    te.wait_ge(S.pc, 1)
    te.wait_ge(S.pscale, 1)
    for o, (ps, mm) in enumerate(((T.ps0, S.mm0), (T.ps1, S.mm1))):
        te.matmul_mx(ps[:, 0:LO], T.wq[:, LO * o:LO * o + LO], T.ws[:, LO * o:LO * o + LO], T.mq[:, 0:LO],
                     T.ms[:, 0:LO], True, True).then_inc(mm, 1)
    v.wait_ge(S.mm0, 1)
    v.tensor_copy(T.ysb[:, 0:LO], T.ps0[:, 0:LO]).then_inc(S.cp0, 1)
    sc.wait_ge(S.mm1, 1)
    sc.activation(T.ysb[:, LO:2 * LO], T.ps1[:, 0:LO], ActivationFunctionType.Copy).then_inc(S.cp1, 1)
    sy.wait_ge(S.cp0, 1)
    sy.dma_start(T.y[:, 0:LO], T.ysb[:, 0:LO]).then_inc(S.st0, 16)
    sc.wait_ge(S.cp1, 1)
    sc.dma_start(T.y[:, LO:2 * LO], T.ysb[:, LO:2 * LO]).then_inc(S.st1, 16)
    sy.wait_ge(S.st0, 16)
    sc.wait_ge(S.st1, 16)
    g.wait_ge(S.left, left[0])
